import numpy as np, ml_dtypes
CORES = [16,17,18,19,150,151]
N = 6
T, CAP = 8192, 512
def entries(a): return a.T.reshape(-1)
def pack(v, P): return np.ascontiguousarray(np.asarray(v, np.int32).reshape(-1, P).T)
def lists(rng, how):
    L = rng.integers(0, T, (N, N, CAP))
    if how == "alike": L[:] = rng.integers(0, T, (N, N, 1))
    if how == "distinct": L = np.stack([np.stack([rng.permutation(T)[:CAP] for d in range(N)]) for r in range(N)])
    if how == "sorted": L = np.sort(L, axis=2)
    if how == "edge": L = np.where(rng.random((N, N, CAP)) < 0.5, 0, T - 1)
    return {"l": np.stack([pack(L[r].reshape(-1), 16) for r in range(N)])}
def setup_inputs(rng):
    return dict({"x": rng.standard_normal((N, 128, T), dtype=np.float32).astype(ml_dtypes.bfloat16)}, **lists(rng, "uniform"))
def setup_inputs_alike(rng):
    d = setup_inputs(rng); d.update(lists(rng, "alike"))
    for k in ("x",): d[k] = (d[k].astype(np.float32) * 1048576.0).astype(d[k].dtype)
    return d
def setup_inputs_distinct(rng):
    d = setup_inputs(rng); d.update(lists(rng, "distinct"))
    for k in ("x",): d[k] = (d[k].astype(np.float32) * (1 / 1024.0)).astype(d[k].dtype)
    return d
def setup_inputs_edge(rng):
    d = setup_inputs(rng); d.update(lists(rng, "edge"))
    return d
def setup_inputs_sorted(rng):
    d = setup_inputs(rng); d.update(lists(rng, "sorted"))
    return d
def check_inputs(x):
    bad = []
    if x["l"].min() < 0 or x["l"].max() >= T: bad.append("l out of range")
    return bad
def reference(x, l):
    y = np.zeros((N, 128, N * CAP), x.dtype)
    for r in range(N):
        L = entries(l[r])
        for d in range(N): y[d][:, CAP * r:CAP * r + CAP] = x[r][:, L[CAP * d:CAP * d + CAP]]
    return {"y": y}

@@ -1,0 +1,123 @@
+from concourse.mybir import AluOpType, ActivationFunctionType
+
+N, COLS, CAP = 6, 8192, 512
+KO = CAP // 16
+HALF = CAP // 2
+
+SCRATCH = {
+    "xs": ("sbuf", [128, COLS], "bfloat16"),
+    "snd": ("sbuf", [128, N * CAP], "bfloat16"),
+    "land": ("sbuf", [128, N * CAP], "bfloat16"),
+    "l32": ("sbuf", [128, N * KO], "int32"),
+    "lf": ("sbuf", [128, N * KO], "float32"),
+    "sel": ("sbuf", [128, 128], "float32"),
+    "rep": ("psum", [128, N * KO], "float32"),
+    "off": ("sbuf", [128, N * KO], "uint16"),
+}
+SEMAPHORES = (["ll", "xl", "c1", "c2", "c3", "c4", "c5", "sent", "st1", "st2"]
+              + ["g%d" % d for d in range(N)] + ["a%d" % s for s in range(N)])
+
+
+def _same_chip(topo, a, b):
+    return topo.host(a) == topo.host(b) and topo.chip(a) == topo.chip(b)
+
+
+def _count(m):
+    return bin(m).count("1")
+
+
+def _order(T, topo, r):
+    cores = T.cores
+    group = [q for q in range(N) if _same_chip(topo, cores[q], cores[r])]
+    far = [q for q in range(N) if q not in group]
+    i = group.index(r)
+    k = i * len(far) // len(group)
+    far = far[k:] + far[:k]
+    near = [group[(i + j) % len(group)] for j in range(1, len(group))]
+    return far, near
+
+
+def _mask(T, topo, s, d):
+    cores = T.cores
+    m = topo.mask(cores[s], cores[d])
+    if _same_chip(topo, cores[s], cores[d]):
+        for q in range(N):
+            if not _same_chip(topo, cores[s], cores[q]):
+                rest = m & ~topo.mask(cores[s], cores[q])
+                if rest:
+                    m = rest
+    return m
+
+
+def _stores(T, topo, r, sources):
+    slot = {}
+    for s in sources:
+        far, near = _order(T, topo, s)
+        slot[s] = (far + near).index(r)
+    out = []
+    for s in sorted(sources, key=lambda q: (slot[q], q)):
+        if out and slot[out[-1][-1]] == slot[s] and out[-1][-1] + 1 == s:
+            out[-1].append(s)
+        else:
+            out.append([s])
+    return out
+
+
+def rank_program(g, core, T, topo):
+    r = T.rank_of(core)
+    if r is None:
+        return
+    S = T.sem
+    cores = T.cores
+    far, near = _order(T, topo, r)
+
+    g.sync.dma_start(T.l32[0:16, :], T.l[:, :]).then_inc(S.ll, 16)
+    g.scalar.dma_start(T.xs[64:128, :], T.x[64:128, :]).then_inc(S.xl, 16)
+    g.sync.dma_start(T.xs[0:64, :], T.x[0:64, :]).then_inc(S.xl, 16)
+
+    g.vector.memset(T.sel[0:16, :], 1.0).then_inc(S.c1, 1)
+    g.wait_ge(S.c1, 1)
+    g.affine_select(T.sel[0:16, :], T.sel[0:16, :], [[0, 8], [-1, 16]], AluOpType.is_equal, 0.0, 0, 1).then_inc(S.c2, 1)
+    g.vector.wait_ge(S.ll, 16)
+    g.vector.tensor_copy(T.lf[0:16, :], T.l32[0:16, :]).then_inc(S.c3, 1)
+    g.tensor.wait_ge(S.c2, 1)
+    g.tensor.wait_ge(S.c3, 1)
+    g.tensor.matmul(T.rep[:, :], T.sel[0:16, :], T.lf[0:16, :], True, True).then_inc(S.c4, 1)
+    g.vector.wait_ge(S.c4, 1)
+    g.vector.tensor_copy(T.off[:, :], T.rep[:, :]).then_inc(S.c5, 1)
+
+    for q in (g.vector, g.scalar):
+        q.wait_ge(S.c5, 1)
+        q.wait_ge(S.xl, 32)
+    for d in far + near + [r]:
+        buf = T.land if d == r else T.snd
+        a, o = CAP * d, KO * d
+        g.vector.tensor_copy(buf[:, a:a + HALF],
+                             T.xs[:, 0:COLS].indirect(T.off[:, o:o + KO // 2])).then_inc(S["g%d" % d], 1)
+        g.scalar.activation(buf[:, a + HALF:a + CAP],
+                            T.xs[:, 0:COLS].indirect(T.off[:, o + KO // 2:o + KO]),
+                            ActivationFunctionType.Copy).then_inc(S["g%d" % d], 1)
+
+    sent = 0
+    for d in far + near:
+        g.wait_ge(S["g%d" % d], 2)
+        rid, pid = topo.addr(cores[d], core)
+        m = _mask(T, topo, r, d)
+        g.remote_dma(out_ap=T.land[:, CAP * r:CAP * r + CAP], in_ap=T.snd[:, CAP * d:CAP * d + CAP],
+                     remote_sem=S["a%d" % r], local_sem=S.sent, pid=pid, routing_id=rid, dma_engine_mask=m)
+        sent += _count(m)
+    g.wait_ge(S.sent, sent)
+
+    for q, sem, sources, own in ((g.sync, S.st1, far, False), (g.scalar, S.st2, near, True)):
+        n = 0
+        for run in _stores(T, topo, r, sources):
+            for s in run:
+                q.wait_ge(S["a%d" % s], _count(_mask(T, topo, s, r)))
+            lo, hi = CAP * run[0], CAP * run[-1] + CAP
+            q.dma_start(T.y[:, lo:hi], T.land[:, lo:hi]).then_inc(sem, 16)
+            n += 16
+        if own:
+            q.wait_ge(S["g%d" % r], 2)
+            q.dma_start(T.y[:, CAP * r:CAP * r + CAP], T.land[:, CAP * r:CAP * r + CAP]).then_inc(sem, 16)
+            n += 16
+        q.wait_ge(sem, n)

@@ -1,6 +1,7 @@
 from concourse.mybir import AluOpType, ActivationFunctionType
 
 N, COLS, CAP = 6, 8192, 512
+WORLD = 256
 KO = CAP // 16
 HALF = CAP // 2
 
@@ -26,7 +27,7 @@ def _count(m):
     return bin(m).count("1")
 
 
-def _order(T, topo, r):
+def _route(T, topo, r):
     cores = T.cores
     group = [q for q in range(N) if _same_chip(topo, cores[q], cores[r])]
     far = [q for q in range(N) if q not in group]
@@ -34,42 +35,73 @@ def _order(T, topo, r):
     k = i * len(far) // len(group)
     far = far[k:] + far[:k]
     near = [group[(i + j) % len(group)] for j in range(1, len(group))]
-    return far, near
+    pool = [c for c in range(WORLD)
+            if T.rank_of(c) is None and _same_chip(topo, c, cores[r]) and topo.die(c) != topo.die(cores[r])
+            and all(topo.may_write(c, cores[d]) for d in far)]
+    via = {}
+    if (i * len(far)) % len(group) == 0 and k < len(pool):
+        via[far[0]] = pool[k]
+    return far, near, via
 
 
-def _mask(T, topo, s, d):
+def _near_mask(T, topo, s, to):
     cores = T.cores
-    m = topo.mask(cores[s], cores[d])
-    if _same_chip(topo, cores[s], cores[d]):
-        for q in range(N):
-            if not _same_chip(topo, cores[s], cores[q]):
-                rest = m & ~topo.mask(cores[s], cores[q])
-                if rest:
-                    m = rest
+    m = topo.mask(cores[s], to)
+    for q in range(N):
+        if not _same_chip(topo, cores[s], cores[q]):
+            rest = m & ~topo.mask(cores[s], cores[q])
+            if rest:
+                m = rest
     return m
 
 
+def _arrives(T, topo, s, r):
+    far, near, via = _route(T, topo, s)
+    if r in near:
+        return _count(_near_mask(T, topo, s, T.cores[r]))
+    return _count(topo.mask(via.get(r, T.cores[s]), T.cores[r]))
+
+
 def _stores(T, topo, r, sources):
-    slot = {}
+    due = {}
     for s in sources:
-        far, near = _order(T, topo, s)
-        slot[s] = (far + near).index(r)
+        far, near, via = _route(T, topo, s)
+        due[s] = (1 if r in via else 0, (far + near).index(r))
     out = []
-    for s in sorted(sources, key=lambda q: (slot[q], q)):
-        if out and slot[out[-1][-1]] == slot[s] and out[-1][-1] + 1 == s:
+    for s in sorted(sources, key=lambda q: (due[q], q)):
+        if out and due[out[-1][-1]] == due[s] and out[-1][-1] + 1 == s:
             out[-1].append(s)
         else:
             out.append([s])
     return out
 
 
+def _relay(g, core, T, topo):
+    S = T.sem
+    sent = 0
+    for s in range(N):
+        far, near, via = _route(T, topo, s)
+        for d in far:
+            if via.get(d) != core:
+                continue
+            g.wait_ge(S["g%d" % d], _count(_near_mask(T, topo, s, core)))
+            rid, pid = topo.addr(T.cores[d], core)
+            m = topo.mask(core, T.cores[d])
+            g.remote_dma(out_ap=T.land[:, CAP * s:CAP * s + CAP], in_ap=T.snd[:, CAP * d:CAP * d + CAP],
+                         remote_sem=S["a%d" % s], local_sem=S.sent, pid=pid, routing_id=rid, dma_engine_mask=m)
+            sent += _count(m)
+    if sent:
+        g.wait_ge(S.sent, sent)
+
+
 def rank_program(g, core, T, topo):
     r = T.rank_of(core)
     if r is None:
+        _relay(g, core, T, topo)
         return
     S = T.sem
     cores = T.cores
-    far, near = _order(T, topo, r)
+    far, near, via = _route(T, topo, r)
 
     g.sync.dma_start(T.l32[0:16, :], T.l[:, :]).then_inc(S.ll, 16)
     g.scalar.dma_start(T.xs[64:128, :], T.x[64:128, :]).then_inc(S.xl, 16)
@@ -101,10 +133,14 @@ def rank_program(g, core, T, topo):
     sent = 0
     for d in far + near:
         g.wait_ge(S["g%d" % d], 2)
-        rid, pid = topo.addr(cores[d], core)
-        m = _mask(T, topo, r, d)
-        g.remote_dma(out_ap=T.land[:, CAP * r:CAP * r + CAP], in_ap=T.snd[:, CAP * d:CAP * d + CAP],
-                     remote_sem=S["a%d" % r], local_sem=S.sent, pid=pid, routing_id=rid, dma_engine_mask=m)
+        blk = T.snd[:, CAP * d:CAP * d + CAP]
+        if d in via:
+            to, out, sem, m = via[d], blk, S["g%d" % d], _near_mask(T, topo, r, via[d])
+        else:
+            to, out, sem = cores[d], T.land[:, CAP * r:CAP * r + CAP], S["a%d" % r]
+            m = _near_mask(T, topo, r, to) if d in near else topo.mask(core, to)
+        rid, pid = topo.addr(to, core)
+        g.remote_dma(out_ap=out, in_ap=blk, remote_sem=sem, local_sem=S.sent, pid=pid, routing_id=rid, dma_engine_mask=m)
         sent += _count(m)
     g.wait_ge(S.sent, sent)
 
@@ -112,7 +148,7 @@ def rank_program(g, core, T, topo):
         n = 0
         for run in _stores(T, topo, r, sources):
             for s in run:
-                q.wait_ge(S["a%d" % s], _count(_mask(T, topo, s, r)))
+                q.wait_ge(S["a%d" % s], _arrives(T, topo, s, r))
             lo, hi = CAP * run[0], CAP * run[-1] + CAP
             q.dma_start(T.y[:, lo:hi], T.land[:, lo:hi]).then_inc(sem, 16)
             n += 16

@@ -4,11 +4,14 @@ N, COLS, CAP = 6, 8192, 512
 WORLD = 256
 KO = CAP // 16
 HALF = CAP // 2
+DIRECT, BY_DIE, BY_MATE = 0, 1, 2
 
 SCRATCH = {
     "xs": ("sbuf", [128, COLS], "bfloat16"),
     "snd": ("sbuf", [128, N * CAP], "bfloat16"),
     "land": ("sbuf", [128, N * CAP], "bfloat16"),
+    "rly": ("dram", [2, 128, HALF], "bfloat16"),
+    "lnd": ("dram", [2 * N, 128, HALF], "bfloat16"),
     "l32": ("sbuf", [128, N * KO], "int32"),
     "lf": ("sbuf", [128, N * KO], "float32"),
     "sel": ("sbuf", [128, 128], "float32"),
@@ -16,7 +19,9 @@ SCRATCH = {
     "off": ("sbuf", [128, N * KO], "uint16"),
 }
 SEMAPHORES = (["ll", "xl", "c1", "c2", "c3", "c4", "c5", "sent", "st1", "st2"]
-              + ["g%d" % d for d in range(N)] + ["a%d" % s for s in range(N)])
+              + ["g%d" % d for d in range(N)] + ["k%d" % d for d in range(N)]
+              + ["a%d" % s for s in range(N)] + ["b%d" % s for s in range(N)])
+_PLANS = {}
 
 
 def _same_chip(topo, a, b):
@@ -27,49 +32,76 @@ def _count(m):
     return bin(m).count("1")
 
 
-def _route(T, topo, r):
+def _mate_pool(T, topo, me, far):
     cores = T.cores
-    group = [q for q in range(N) if _same_chip(topo, cores[q], cores[r])]
-    far = [q for q in range(N) if q not in group]
-    i = group.index(r)
-    k = i * len(far) // len(group)
-    far = far[k:] + far[:k]
-    near = [group[(i + j) % len(group)] for j in range(1, len(group))]
     pool = [c for c in range(WORLD)
-            if T.rank_of(c) is None and _same_chip(topo, c, cores[r]) and topo.die(c) != topo.die(cores[r])
-            and all(topo.may_write(c, cores[d]) for d in far)]
-    via = {}
-    if (i * len(far)) % len(group) == 0 and k < len(pool):
-        via[far[0]] = pool[k]
-    return far, near, via
+            if T.rank_of(c) is None and topo.may_write(me, c)
+            and all(topo.mates(c, cores[d]) and topo.may_write(c, cores[d]) for d in far)]
+    return sorted(pool, key=lambda c: topo.die(c) != topo.die(cores[far[0]]))
 
 
-def _near_mask(T, topo, s, to):
+def _plan(T, topo, r):
+    if r in _PLANS:
+        return _PLANS[r]
     cores = T.cores
-    m = topo.mask(cores[s], to)
-    for q in range(N):
-        if not _same_chip(topo, cores[s], cores[q]):
-            rest = m & ~topo.mask(cores[s], cores[q])
-            if rest:
-                m = rest
-    return m
+    me = cores[r]
+    group = [q for q in range(N) if _same_chip(topo, cores[q], me)]
+    base = [q for q in range(N) if q not in group]
+    per = len(base) // 2
+    pool = [c for c in range(WORLD)
+            if T.rank_of(c) is None and _same_chip(topo, c, me) and topo.die(c) != topo.die(me)
+            and all(topo.may_write(c, cores[d]) for d in base)]
+    able = [q for q in group if _mate_pool(T, topo, cores[q], base)][-1:]
+    used = 0
+    far, way, to = base, {}, {}
+    for i, s in enumerate(group):
+        k = (i * per) % len(base)
+        far, way, to = base[k:] + base[:k], {}, {}
+        for j, d in enumerate(far[:per]):
+            if s in able and j == 0:
+                way[d], to[d] = BY_MATE, _mate_pool(T, topo, cores[s], base)[0]
+            else:
+                way[d], to[d] = BY_DIE, pool[used]
+                used += 1
+        if s == r:
+            break
+    i = group.index(r)
+    near = [group[(i + j) % len(group)] for j in range(1, len(group))]
+    full = topo.mask(me, cores[near[0]])
+    lo = full
+    for d in far:
+        lo &= topo.mask(me, cores[d])
+    hi = full & ~lo
+    plan = []
+    for d in sorted(far, key=lambda q: -way.get(q, DIRECT)):
+        w = way.get(d, DIRECT)
+        plan.append((d, to.get(d, cores[d]), hi if w == BY_DIE else lo & topo.mask(me, to.get(d, cores[d])), w))
+    for d in near:
+        plan.append((d, cores[d], hi, DIRECT))
+    _PLANS[r] = plan
+    return plan
+
+
+def _leg(T, topo, s, r):
+    for n, e in enumerate(_plan(T, topo, s)):
+        if e[0] == r:
+            return n, e
+    return None
 
 
 def _arrives(T, topo, s, r):
-    far, near, via = _route(T, topo, s)
-    if r in near:
-        return _count(_near_mask(T, topo, s, T.cores[r]))
-    return _count(topo.mask(via.get(r, T.cores[s]), T.cores[r]))
+    n, (d, to, m, w) = _leg(T, topo, s, r)
+    return _count(m) if w == DIRECT else _count(topo.mask(to, T.cores[r]))
 
 
 def _stores(T, topo, r, sources):
     due = {}
     for s in sources:
-        far, near, via = _route(T, topo, s)
-        due[s] = (1 if r in via else 0, (far + near).index(r))
+        n, e = _leg(T, topo, s, r)
+        due[s] = (e[3], n)
     out = []
     for s in sorted(sources, key=lambda q: (due[q], q)):
-        if out and due[out[-1][-1]] == due[s] and out[-1][-1] + 1 == s:
+        if out and due[s][0] == DIRECT and due[out[-1][-1]] == due[s] and out[-1][-1] + 1 == s:
             out[-1].append(s)
         else:
             out.append([s])
@@ -80,16 +112,16 @@ def _relay(g, core, T, topo):
     S = T.sem
     sent = 0
     for s in range(N):
-        far, near, via = _route(T, topo, s)
-        for d in far:
-            if via.get(d) != core:
+        for d, to, hm, w in _plan(T, topo, s):
+            if w == DIRECT or to != core:
                 continue
-            g.wait_ge(S["g%d" % d], _count(_near_mask(T, topo, s, core)))
             rid, pid = topo.addr(T.cores[d], core)
             m = topo.mask(core, T.cores[d])
-            g.remote_dma(out_ap=T.land[:, CAP * s:CAP * s + CAP], in_ap=T.snd[:, CAP * d:CAP * d + CAP],
-                         remote_sem=S["a%d" % s], local_sem=S.sent, pid=pid, routing_id=rid, dma_engine_mask=m)
-            sent += _count(m)
+            for h in range(2):
+                g.wait_ge(S["gk"[h] + "%d" % d], _count(hm))
+                g.remote_dma(out_ap=T.lnd[2 * s + h], in_ap=T.rly[h],
+                             remote_sem=S["ab"[h] + "%d" % s], local_sem=S.sent, pid=pid, routing_id=rid, dma_engine_mask=m)
+                sent += _count(m)
     if sent:
         g.wait_ge(S.sent, sent)
 
@@ -101,7 +133,9 @@ def rank_program(g, core, T, topo):
         return
     S = T.sem
     cores = T.cores
-    far, near, via = _route(T, topo, r)
+    plan = _plan(T, topo, r)
+    far = [q for q in range(N) if not _same_chip(topo, cores[q], core)]
+    near = [q for q in range(N) if q != r and q not in far]
 
     g.sync.dma_start(T.l32[0:16, :], T.l[:, :]).then_inc(S.ll, 16)
     g.scalar.dma_start(T.xs[64:128, :], T.x[64:128, :]).then_inc(S.xl, 16)
@@ -121,39 +155,55 @@ def rank_program(g, core, T, topo):
     for q in (g.vector, g.scalar):
         q.wait_ge(S.c5, 1)
         q.wait_ge(S.xl, 32)
-    for d in far + near + [r]:
+    for d, w in [(e[0], e[3]) for e in plan] + [(r, DIRECT)]:
         buf = T.land if d == r else T.snd
-        a, o = CAP * d, KO * d
-        g.vector.tensor_copy(buf[:, a:a + HALF],
-                             T.xs[:, 0:COLS].indirect(T.off[:, o:o + KO // 2])).then_inc(S["g%d" % d], 1)
-        g.scalar.activation(buf[:, a + HALF:a + CAP],
-                            T.xs[:, 0:COLS].indirect(T.off[:, o + KO // 2:o + KO]),
-                            ActivationFunctionType.Copy).then_inc(S["g%d" % d], 1)
+        pieces = [(0, CAP, "g")] if w == DIRECT else [(0, HALF, "g"), (HALF, HALF, "k")]
+        for p0, width, name in pieces:
+            a, o, e = CAP * d + p0, KO * d + p0 // 16, width // 2
+            g.vector.tensor_copy(buf[:, a:a + e],
+                                 T.xs[:, 0:COLS].indirect(T.off[:, o:o + e // 16])).then_inc(S[name + "%d" % d], 1)
+            g.scalar.activation(buf[:, a + e:a + 2 * e],
+                                T.xs[:, 0:COLS].indirect(T.off[:, o + e // 16:o + e // 8]),
+                                ActivationFunctionType.Copy).then_inc(S[name + "%d" % d], 1)
 
     sent = 0
-    for d in far + near:
-        g.wait_ge(S["g%d" % d], 2)
-        blk = T.snd[:, CAP * d:CAP * d + CAP]
-        if d in via:
-            to, out, sem, m = via[d], blk, S["g%d" % d], _near_mask(T, topo, r, via[d])
-        else:
-            to, out, sem = cores[d], T.land[:, CAP * r:CAP * r + CAP], S["a%d" % r]
-            m = _near_mask(T, topo, r, to) if d in near else topo.mask(core, to)
+    for d, to, m, w in plan:
         rid, pid = topo.addr(to, core)
-        g.remote_dma(out_ap=out, in_ap=blk, remote_sem=sem, local_sem=S.sent, pid=pid, routing_id=rid, dma_engine_mask=m)
-        sent += _count(m)
+        if w == DIRECT:
+            g.wait_ge(S["g%d" % d], 2)
+            g.remote_dma(out_ap=T.land[:, CAP * r:CAP * r + CAP], in_ap=T.snd[:, CAP * d:CAP * d + CAP],
+                         remote_sem=S["a%d" % r], local_sem=S.sent, pid=pid, routing_id=rid, dma_engine_mask=m)
+            sent += _count(m)
+            continue
+        for h in range(2):
+            sem = S["gk"[h] + "%d" % d]
+            g.wait_ge(sem, 2)
+            a = CAP * d + HALF * h
+            g.remote_dma(out_ap=T.rly[h], in_ap=T.snd[:, a:a + HALF], remote_sem=sem, local_sem=S.sent,
+                         pid=pid, routing_id=rid, dma_engine_mask=m)
+            sent += _count(m)
     g.wait_ge(S.sent, sent)
 
-    for q, sem, sources, own in ((g.sync, S.st1, far, False), (g.scalar, S.st2, near, True)):
+    by_die = [s for s in far if _leg(T, topo, s, r)[1][3] == BY_DIE]
+    first = _stores(T, topo, r, [s for s in far if s not in by_die])
+    second = _stores(T, topo, r, near) + [[r]] + _stores(T, topo, r, by_die)
+    for q, sem, runs in ((g.sync, S.st1, first), (g.scalar, S.st2, second)):
         n = 0
-        for run in _stores(T, topo, r, sources):
+        for run in runs:
+            s = run[0]
+            if s != r and _leg(T, topo, s, r)[1][3] != DIRECT:
+                for h in range(2):
+                    q.wait_ge(S["ab"[h] + "%d" % s], _arrives(T, topo, s, r))
+                    a = CAP * s + HALF * h
+                    q.dma_start(T.y[:, a:a + HALF], T.lnd[2 * s + h]).then_inc(sem, 16)
+                    n += 16
+                continue
             for s in run:
-                q.wait_ge(S["a%d" % s], _arrives(T, topo, s, r))
+                if s == r:
+                    q.wait_ge(S["g%d" % r], 2)
+                else:
+                    q.wait_ge(S["a%d" % s], _arrives(T, topo, s, r))
             lo, hi = CAP * run[0], CAP * run[-1] + CAP
             q.dma_start(T.y[:, lo:hi], T.land[:, lo:hi]).then_inc(sem, 16)
-            n += 16
-        if own:
-            q.wait_ge(S["g%d" % r], 2)
-            q.dma_start(T.y[:, CAP * r:CAP * r + CAP], T.land[:, CAP * r:CAP * r + CAP]).then_inc(sem, 16)
             n += 16
         q.wait_ge(sem, n)

from concourse.mybir import AluOpType, ActivationFunctionType

N, COLS, CAP = 6, 8192, 512
WORLD = 256
KO = CAP // 16
HALF = CAP // 2
DIRECT, BY_DIE, BY_MATE = 0, 1, 2

SCRATCH = {
    "xs": ("sbuf", [128, COLS], "bfloat16"),
    "snd": ("sbuf", [128, N * CAP], "bfloat16"),
    "land": ("sbuf", [128, N * CAP], "bfloat16"),
    "rly": ("dram", [2, 128, HALF], "bfloat16"),
    "lnd": ("dram", [2 * N, 128, HALF], "bfloat16"),
    "l32": ("sbuf", [128, N * KO], "int32"),
    "lf": ("sbuf", [128, N * KO], "float32"),
    "sel": ("sbuf", [128, 128], "float32"),
    "rep": ("psum", [128, N * KO], "float32"),
    "off": ("sbuf", [128, N * KO], "uint16"),
}
SEMAPHORES = (["ll", "xl", "c1", "c2", "c3", "c4", "c5", "sent", "st1", "st2"]
              + ["g%d" % d for d in range(N)] + ["k%d" % d for d in range(N)]
              + ["a%d" % s for s in range(N)] + ["b%d" % s for s in range(N)])
_PLANS = {}


def _same_chip(topo, a, b):
    return topo.host(a) == topo.host(b) and topo.chip(a) == topo.chip(b)


def _count(m):
    return bin(m).count("1")


def _mate_pool(T, topo, me, far):
    cores = T.cores
    pool = [c for c in range(WORLD)
            if T.rank_of(c) is None and topo.may_write(me, c)
            and all(topo.mates(c, cores[d]) and topo.may_write(c, cores[d]) for d in far)]
    return sorted(pool, key=lambda c: topo.die(c) != topo.die(cores[far[0]]))


def _plan(T, topo, r):
    if r in _PLANS:
        return _PLANS[r]
    cores = T.cores
    me = cores[r]
    group = [q for q in range(N) if _same_chip(topo, cores[q], me)]
    base = [q for q in range(N) if q not in group]
    per = len(base) // 2
    pool = [c for c in range(WORLD)
            if T.rank_of(c) is None and _same_chip(topo, c, me) and topo.die(c) != topo.die(me)
            and all(topo.may_write(c, cores[d]) for d in base)]
    able = [q for q in group if _mate_pool(T, topo, cores[q], base)][-1:]
    used = 0
    far, way, to = base, {}, {}
    for i, s in enumerate(group):
        k = (i * per) % len(base)
        far, way, to = base[k:] + base[:k], {}, {}
        for j, d in enumerate(far[:per]):
            if s in able and j == 0:
                way[d], to[d] = BY_MATE, _mate_pool(T, topo, cores[s], base)[0]
            else:
                way[d], to[d] = BY_DIE, pool[used]
                used += 1
        if s == r:
            break
    i = group.index(r)
    near = [group[(i + j) % len(group)] for j in range(1, len(group))]
    full = topo.mask(me, cores[near[0]])
    lo = full
    for d in far:
        lo &= topo.mask(me, cores[d])
    hi = full & ~lo
    plan = []
    for d in sorted(far, key=lambda q: -way.get(q, DIRECT)):
        w = way.get(d, DIRECT)
        plan.append((d, to.get(d, cores[d]), hi if w == BY_DIE else lo & topo.mask(me, to.get(d, cores[d])), w))
    for d in near:
        plan.append((d, cores[d], hi, DIRECT))
    _PLANS[r] = plan
    return plan


def _leg(T, topo, s, r):
    for n, e in enumerate(_plan(T, topo, s)):
        if e[0] == r:
            return n, e
    return None


def _arrives(T, topo, s, r):
    n, (d, to, m, w) = _leg(T, topo, s, r)
    return _count(m) if w == DIRECT else _count(topo.mask(to, T.cores[r]))


def _stores(T, topo, r, sources):
    due = {}
    for s in sources:
        n, e = _leg(T, topo, s, r)
        due[s] = (e[3], n)
    out = []
    for s in sorted(sources, key=lambda q: (due[q], q)):
        if out and due[s][0] == DIRECT and due[out[-1][-1]] == due[s] and out[-1][-1] + 1 == s:
            out[-1].append(s)
        else:
            out.append([s])
    return out


def _relay(g, core, T, topo):
    S = T.sem
    sent = 0
    for s in range(N):
        for d, to, hm, w in _plan(T, topo, s):
            if w == DIRECT or to != core:
                continue
            rid, pid = topo.addr(T.cores[d], core)
            m = topo.mask(core, T.cores[d])
            for h in range(2):
                g.wait_ge(S["gk"[h] + "%d" % d], _count(hm))
                g.remote_dma(out_ap=T.lnd[2 * s + h], in_ap=T.rly[h],
                             remote_sem=S["ab"[h] + "%d" % s], local_sem=S.sent, pid=pid, routing_id=rid, dma_engine_mask=m)
                sent += _count(m)
    if sent:
        g.wait_ge(S.sent, sent)


def rank_program(g, core, T, topo):
    r = T.rank_of(core)
    if r is None:
        _relay(g, core, T, topo)
        return
    S = T.sem
    cores = T.cores
    plan = _plan(T, topo, r)
    far = [q for q in range(N) if not _same_chip(topo, cores[q], core)]
    near = [q for q in range(N) if q != r and q not in far]

    g.sync.dma_start(T.l32[0:16, :], T.l[:, :]).then_inc(S.ll, 16)
    g.scalar.dma_start(T.xs[64:128, :], T.x[64:128, :]).then_inc(S.xl, 16)
    g.sync.dma_start(T.xs[0:64, :], T.x[0:64, :]).then_inc(S.xl, 16)

    g.vector.memset(T.sel[0:16, :], 1.0).then_inc(S.c1, 1)
    g.wait_ge(S.c1, 1)
    g.affine_select(T.sel[0:16, :], T.sel[0:16, :], [[0, 8], [-1, 16]], AluOpType.is_equal, 0.0, 0, 1).then_inc(S.c2, 1)
    g.vector.wait_ge(S.ll, 16)
    g.vector.tensor_copy(T.lf[0:16, :], T.l32[0:16, :]).then_inc(S.c3, 1)
    g.tensor.wait_ge(S.c2, 1)
    g.tensor.wait_ge(S.c3, 1)
    g.tensor.matmul(T.rep[:, :], T.sel[0:16, :], T.lf[0:16, :], True, True).then_inc(S.c4, 1)
    g.vector.wait_ge(S.c4, 1)
    g.vector.tensor_copy(T.off[:, :], T.rep[:, :]).then_inc(S.c5, 1)

    for q in (g.vector, g.scalar):
        q.wait_ge(S.c5, 1)
        q.wait_ge(S.xl, 32)
    for d, w in [(e[0], e[3]) for e in plan] + [(r, DIRECT)]:
        buf = T.land if d == r else T.snd
        pieces = [(0, CAP, "g")] if w == DIRECT else [(0, HALF, "g"), (HALF, HALF, "k")]
        for p0, width, name in pieces:
            a, o, e = CAP * d + p0, KO * d + p0 // 16, width // 2
            g.vector.tensor_copy(buf[:, a:a + e],
                                 T.xs[:, 0:COLS].indirect(T.off[:, o:o + e // 16])).then_inc(S[name + "%d" % d], 1)
            g.scalar.activation(buf[:, a + e:a + 2 * e],
                                T.xs[:, 0:COLS].indirect(T.off[:, o + e // 16:o + e // 8]),
                                ActivationFunctionType.Copy).then_inc(S[name + "%d" % d], 1)

    sent = 0
    for d, to, m, w in plan:
        rid, pid = topo.addr(to, core)
        if w == DIRECT:
            g.wait_ge(S["g%d" % d], 2)
            g.remote_dma(out_ap=T.land[:, CAP * r:CAP * r + CAP], in_ap=T.snd[:, CAP * d:CAP * d + CAP],
                         remote_sem=S["a%d" % r], local_sem=S.sent, pid=pid, routing_id=rid, dma_engine_mask=m)
            sent += _count(m)
            continue
        for h in range(2):
            sem = S["gk"[h] + "%d" % d]
            g.wait_ge(sem, 2)
            a = CAP * d + HALF * h
            g.remote_dma(out_ap=T.rly[h], in_ap=T.snd[:, a:a + HALF], remote_sem=sem, local_sem=S.sent,
                         pid=pid, routing_id=rid, dma_engine_mask=m)
            sent += _count(m)
    g.wait_ge(S.sent, sent)

    by_die = [s for s in far if _leg(T, topo, s, r)[1][3] == BY_DIE]
    first = _stores(T, topo, r, [s for s in far if s not in by_die])
    second = _stores(T, topo, r, near) + [[r]] + _stores(T, topo, r, by_die)
    for q, sem, runs in ((g.sync, S.st1, first), (g.scalar, S.st2, second)):
        n = 0
        for run in runs:
            s = run[0]
            if s != r and _leg(T, topo, s, r)[1][3] != DIRECT:
                for h in range(2):
                    q.wait_ge(S["ab"[h] + "%d" % s], _arrives(T, topo, s, r))
                    a = CAP * s + HALF * h
                    q.dma_start(T.y[:, a:a + HALF], T.lnd[2 * s + h]).then_inc(sem, 16)
                    n += 16
                continue
            for s in run:
                if s == r:
                    q.wait_ge(S["g%d" % r], 2)
                else:
                    q.wait_ge(S["a%d" % s], _arrives(T, topo, s, r))
            lo, hi = CAP * run[0], CAP * run[-1] + CAP
            q.dma_start(T.y[:, lo:hi], T.land[:, lo:hi]).then_inc(sem, 16)
            n += 16
        q.wait_ge(sem, n)
